import numpy as np
import ml_dtypes


def mxq(x, axis, fmt="e4m3"):
    dtype, down = {"e4m3": (ml_dtypes.float8_e4m3fn, 7), "e5m2": (ml_dtypes.float8_e5m2, 14)}[fmt]
    v = np.moveaxis(np.asarray(x, np.float32).astype(ml_dtypes.bfloat16).astype(np.float64), axis, -1)
    blocks = v.reshape(v.shape[:-1] + (-1, 32))
    amax = np.abs(blocks).max(-1, keepdims=True)
    byte = np.maximum(np.where(amax > 0, np.frexp(amax)[1] - 1 + 127, 0) - down, 1)
    scale = np.exp2(byte - 127.0)
    codes = (blocks / scale).astype(np.float32).astype(dtype).astype(np.float64)
    return np.moveaxis((codes * scale).reshape(v.shape), -1, axis)


WIDE = False


def mx_kscale(k):
    if not WIDE:
        return np.ones(k)
    levels = np.array([10, -10, 5, -5, 0])
    if k % 512:
        return np.exp2(np.random.permutation(np.resize(levels, k // 32))).repeat(32)
    a = np.empty((k // 512, 16))
    for p in range(k // 512):
        a[p, :8] = np.random.permutation(np.resize(levels, 8))
        for g in range(8):
            far = levels[np.abs(levels - a[p, g]) >= 10]
            a[p, g + 8] = far[np.random.randint(len(far))]
    return np.exp2(a.ravel()).repeat(32)


def f64(x):
    return np.asarray(x).astype(np.float64)


def striped(idx):
    return np.tile(idx.reshape(-1, 16).T, (8, 1)).astype(np.uint16)


def unstriped(offs):
    return offs[:16].T.reshape(-1).astype(np.int64)


E2M1 = np.array([0.0, 0.5, 1.0, 1.5, 2.0, 3.0, 4.0, 6.0, -0.0, -0.5, -1.0, -1.5, -2.0, -3.0, -4.0, -6.0])


def pack_weight(w, fmt):
    k, n = w.shape
    w = f64(np.asarray(w, np.float32).astype(ml_dtypes.bfloat16)).reshape(k // 32, 32, n)
    amax = np.abs(w).max(1)
    if fmt == "e4m3":
        byte = np.frexp(amax)[1] - 1 + 127 - 7
    else:
        mant, ex = np.frexp(amax / 6.0)
        byte = np.where(mant > 0.5, ex, ex - 1) + 127
    byte = np.clip(np.where(amax > 0, byte, 1), 1, 254)
    scaled = (w * np.exp2(127.0 - byte)[:, None, :]).reshape(k, n).astype(np.float32)
    by_word = np.ascontiguousarray(scaled.reshape(k // 512, 128, 4, n).transpose(0, 1, 3, 2))
    if fmt == "e4m3":
        words = by_word.astype(ml_dtypes.float8_e4m3fn).view(np.uint8)
    else:
        c = by_word.astype(ml_dtypes.float4_e2m1fn).view(np.uint8) & 0xF
        words = (c[..., 0::2] | (c[..., 1::2] << 4)).reshape(k // 512, 128, 2 * n)
    return np.ascontiguousarray(words), np.ascontiguousarray(byte.astype(np.uint8).reshape(k // 512, 16, n))


def unpack_weight(words, scales, fmt):
    g, _, n = scales.shape
    words = np.ascontiguousarray(words).reshape(g, 128, n, -1)
    if fmt == "e4m3":
        vals = words.view(ml_dtypes.float8_e4m3fn).astype(np.float64)
    else:
        nib = np.empty((g, 128, n, 4), np.uint8)
        nib[..., 0::2] = words & 0xF
        nib[..., 1::2] = words >> 4
        vals = E2M1[nib]
    vals = vals * np.repeat(np.exp2(scales.astype(np.float64) - 127.0), 8, axis=1)[..., None]
    return vals.transpose(0, 1, 3, 2).reshape(g * 512, n)


def gelu(v):
    return 0.5 * v * (1.0 + np.tanh(np.sqrt(2.0 / np.pi) * (v + 0.044715 * v**3)))


K, T, S, H, T2, P = 1536, 4096, 1024, 512, 2048, 1024

def setup_inputs():
    n = np.random.standard_normal
    s = mx_kscale(K)[:, None]
    u = mx_kscale(H)[:, None]
    d = {}
    d["tab_words"], d["tab_scales"] = pack_weight(n((K, T)) * s, "e4m3")
    d["offs"] = striped(np.random.permutation(T)[:S])
    d["offs2"] = striped(np.random.permutation(T2)[:S])
    d["offs3"] = striped(np.random.permutation(T2)[:P])
    d["offs4"] = striped(np.random.permutation(T2)[:P])
    d["w1"] = (n((K, H)) * 0.55 / K**0.5 / s).astype(np.float32)
    d["gain"] = (1.8 * np.exp(0.25 * n(H)) * u[:, 0]).astype(np.float32)
    d["base"] = (0.5 * n((H, S)) * u).astype(np.float32)
    d["wgs"] = np.exp(0.3 * n((128, S))).astype(np.float32)
    d["page0"] = (n((H, T2)) * u).astype(np.float32)
    d["sens"] = np.exp(0.3 * n(H)).astype(np.float32)
    d["w2_words"], d["w2_scales"] = pack_weight(n((H, H)) / H**0.5 / u, "e2m1")
    d["refs"] = (0.9 * np.exp(0.3 * n(H)) / u[:, 0]).astype(np.float32)
    return d

def reference(tab_words, tab_scales, offs, offs2, offs3, offs4, w1, gain, base,
              wgs, page0, sens, w2_words, w2_scales, refs):
    v = unpack_weight(tab_words, tab_scales, "e4m3")[:, unstriped(offs)]
    w2 = unpack_weight(w2_words, w2_scales, "e2m1")
    s1 = mxq(f64(w1), 0, "e4m3").T @ v
    h = f64(gain)[:, None] * np.sin(s1) + f64(base)
    page = f64(page0).copy()
    page[:, unstriped(offs2)] = np.tile(f64(wgs), (H // 128, 1)) * h
    x = np.abs(f64(sens)[:, None] * page[:, unstriped(offs3)])
    y = w2.T @ mxq(x, 0, "e4m3")
    return np.maximum(y, f64(refs)[:, None] * page[:, unstriped(offs4)])

@@ -1,0 +1,289 @@
+import math
+from contextlib import ExitStack
+
+import concourse.mybir as mybir
+from concourse.masks import make_identity
+
+K, T, S, H, T2 = 1536, 4096, 1024, 512, 2048
+FLOPS = 2 * K * H * S + 2 * H * H * S
+
+F32 = mybir.dt.float32
+BF16 = mybir.dt.bfloat16
+I32 = mybir.dt.int32
+U32 = mybir.dt.uint32
+U16 = mybir.dt.uint16
+U8 = mybir.dt.uint8
+FP8X4 = mybir.dt.float8_e4m3fn_x4
+FP4X4 = mybir.dt.float4_e2m1fn_x4
+ALU = mybir.AluOpType
+ACT = mybir.ActivationFunctionType
+
+P = 128
+PACK = 4
+PASSES = K // (P * PACK)
+HALF = 512
+TWO_PI = 2.0 * math.pi
+ROUNDER = 1.5 * 2.0**23
+
+
+def tile_list_bogie_vibration_page_kernel(
+    tc, tab_words, tab_scales, offs, offs2, offs3, offs4, w1, gain, base,
+    wgs, page0, sens, w2_words, w2_scales, refs, out,
+):
+    nc = tc.nc
+    with ExitStack() as ctx:
+        keep = ctx.enter_context(tc.tile_pool(name="keep", bufs=1))
+        big = ctx.enter_context(tc.tile_pool(name="big", bufs=3))
+        work = ctx.enter_context(tc.tile_pool(name="work", bufs=2))
+        psum = ctx.enter_context(tc.psum_pool(name="psum", bufs=2))
+
+        def cols(h):
+            return slice(h * HALF, (h + 1) * HALF)
+
+        def entries(lst, h):
+            return lst[:, h * HALF // 16 : (h + 1) * HALF // 16]
+
+        def block(b):
+            return slice(b * P, (b + 1) * P)
+
+        lists = [keep.tile([P, S // 16], U16, name=f"list{i}") for i in range(4)]
+        tab_sc = keep.tile([P, T], U8, name="tab_sc")
+        w2_sc_raw = keep.tile([P, H], U8, name="w2_sc_raw")
+        nc.vector.memset(tab_sc[:].bitcast(I32), 0)
+        nc.vector.memset(w2_sc_raw[:].bitcast(I32), 0)
+        zero_in = keep.tile([P, 1], F32, name="zero_in")
+        zero = keep.tile([P, 1], F32, name="zero")
+        nc.vector.memset(zero_in[:], 0.0)
+        nc.scalar.activation(zero[:], zero_in[:], ACT.Sin, bias=zero_in[:])
+
+        w2_raw = keep.tile([P, 2 * H], U8, name="w2_raw")
+        gain_sb = keep.tile([P, PACK], F32, name="gain_sb")
+        sens_sb = keep.tile([P, PACK], F32, name="sens_sb")
+        refs_sb = keep.tile([P, PACK], F32, name="refs_sb")
+        ident = keep.tile([P, P], F32, name="ident")
+        make_identity(nc, ident[:])
+
+        w1_raw = [keep.tile([P, PACK, H], F32, name=f"w1_raw{a}") for a in range(PASSES)]
+        tab = [big.tile([P, T], U32, name=f"tab{a}", tag="big") for a in range(PASSES)]
+
+        def load_w1(a):
+            rows = w1[a * P * PACK : (a + 1) * P * PACK, :]
+            nc.sync.dma_start(out=w1_raw[a][:], in_=rows.rearrange("(p j) c -> p j c", j=PACK))
+
+        def load_tab(a, half):
+            words = tab_words[a].rearrange("p n i -> p (n i)").bitcast(I32)
+            c = slice(half * T // 2, (half + 1) * T // 2)
+            nc.sync.dma_start(out=tab[a][:].bitcast(I32)[:, c], in_=words[:, c])
+
+        def load_vec(dst, src):
+            nc.sync.dma_start(out=dst[:], in_=src.rearrange("(p t) -> p t", t=PACK))
+
+        def load_tab_sc(q):
+            nc.sync.dma_start(
+                out=tab_sc[32 * q : 32 * q + 4 * PASSES, :].bitcast(I32),
+                in_=tab_scales[:, 4 * q : 4 * q + 4, :].bitcast(I32),
+            )
+
+        def load_w2_sc(q):
+            nc.sync.dma_start(
+                out=w2_sc_raw[32 * q : 32 * q + 4, :].bitcast(I32),
+                in_=w2_scales[0, 4 * q : 4 * q + 4, :].bitcast(I32),
+            )
+
+        nc.sync.dma_start(lists[0][:], offs)
+        load_w1(0)
+        load_w1(1)
+        nc.sync.dma_start(out=w2_raw[:].bitcast(I32), in_=w2_words[0].bitcast(I32))
+        load_tab(0, 0)
+        load_vec(gain_sb, gain)
+        load_tab(0, 1)
+        load_vec(sens_sb, sens)
+        for a, load_sc in ((1, load_tab_sc), (2, load_w2_sc)):
+            for half in range(2):
+                load_sc(2 * half)
+                load_sc(2 * half + 1)
+                load_tab(a, half)
+        load_w1(2)
+
+        base_t = base.rearrange("(p t) j -> t p j", t=PACK)
+        page_t = page0.rearrange("(p t) m -> t p m", t=PACK)
+        out_t = out.rearrange("(p t) j -> t p j", t=PACK)
+        wgs_q = wgs.rearrange("(q t) j -> q t j", t=PACK)
+        base_sb = [keep.tile([P, S], F32, name=f"base{t}") for t in range(PACK)]
+        page = [keep.tile([P, T2], F32, name=f"page{t}") for t in range(PACK)]
+        wgs_first = keep.tile([P, S], F32, name="wgs_first")
+        wgs_rest = keep.tile([P, PACK - 1, S], F32, name="wgs_rest")
+        wgs_sb = [wgs_first[:]] + [wgs_rest[:, t, :] for t in range(PACK - 1)]
+
+        nc.sync.dma_start(out=base_sb[0][:], in_=base_t[0])
+        nc.sync.dma_start(lists[1][:], offs2)
+        for g in range(4):
+            nc.sync.dma_start(out=wgs_first[32 * g : 32 * g + 32, :], in_=wgs_q[:, 0, :])
+        nc.sync.dma_start(out=page[0][:], in_=page_t[0])
+        nc.sync.dma_start(out=base_sb[1][:], in_=base_t[1])
+        load_vec(refs_sb, refs)
+        nc.sync.dma_start(lists[2][:], offs3)
+        nc.sync.dma_start(lists[3][:], offs4)
+        for g in range(4):
+            nc.sync.dma_start(out=wgs_rest[32 * g : 32 * g + 32, :, :], in_=wgs_q[:, 1:PACK, :])
+        nc.sync.dma_start(out=page[1][:], in_=page_t[1])
+        for t in range(2, PACK):
+            nc.sync.dma_start(out=base_sb[t][:], in_=base_t[t])
+            nc.sync.dma_start(out=page[t][:], in_=page_t[t])
+
+        w2_dealt = keep.tile([P, 2 * H], U8, name="w2_dealt", align_bytes=64)
+        w2_sc = keep.tile([P, H], U8, name="w2_sc", align_bytes=64)
+
+        w1_codes = [keep.tile([P, H], U32, name=f"w1_codes{a}", align_bytes=64) for a in range(PASSES)]
+        w1_sc = [keep.tile([P, H], U8, name=f"w1_sc{a}", align_bytes=64) for a in range(PASSES)]
+        v_codes = [keep.tile([P, S], U32, name=f"v_codes{a}", align_bytes=64) for a in range(PASSES)]
+        v_sc = keep.tile([P, S], U8, name="v_sc", align_bytes=64)
+
+        def quantise_w1(a):
+            src = w1_raw[a][:].rearrange("p j (m t) -> p m t j", t=PACK)
+            first = keep.tile([P, H], BF16, name=f"w1_first{a}", align_bytes=64)
+            rest = keep.tile([P, (PACK - 1) * H], BF16, name=f"w1_rest{a}", align_bytes=64)
+            nc.vector.tensor_copy(out=first[:].rearrange("p (m j) -> p m j", j=PACK), in_=src[:, :, 0, :])
+            nc.scalar.copy(
+                out=rest[:].rearrange("p (t m j) -> p m t j", t=PACK - 1, j=PACK), in_=src[:, :, 1:PACK, :]
+            )
+            nc.vector.quantize_mx(out=w1_codes[a][:, 0:P].bitcast(FP8X4), scales=w1_sc[a][:, 0:P], in_=first[:])
+            return rest
+
+        def quantise_w1_rest(a, rest):
+            for lo, hi in ((1, 2), (2, 4)):
+                nc.vector.quantize_mx(
+                    out=w1_codes[a][:, lo * P : hi * P].bitcast(FP8X4),
+                    scales=w1_sc[a][:, lo * P : hi * P],
+                    in_=rest[:, (lo - 1) * H : (hi - 1) * H],
+                )
+
+        for a in range(PASSES - 1):
+            quantise_w1_rest(a, quantise_w1(a))
+        nc.vector.tensor_copy(v_codes[0][:], tab[0][:].indirect(lists[0][:]))
+        nc.vector.tensor_copy(v_sc[:], tab_sc[:].indirect(lists[0][:]))
+        nc.vector.tensor_copy(v_codes[1][:], tab[1][:].indirect(lists[0][:]))
+        nc.vector.tensor_copy(
+            out=w2_dealt[:].rearrange("p (t m b) -> p t m b", t=PACK, b=2),
+            in_=w2_raw[:].rearrange("p (m t b) -> p t m b", t=PACK, b=2),
+        )
+        nc.vector.tensor_copy(
+            out=w2_sc[:].rearrange("p (t m) -> p t m", t=PACK),
+            in_=w2_sc_raw[:].rearrange("p (m t) -> p t m", t=PACK),
+        )
+        nc.vector.tensor_copy(v_codes[2][:], tab[2][:].indirect(lists[0][:]))
+        last_rest = quantise_w1(PASSES - 1)
+
+        g3 = big.tile([P, PACK, S], F32, name="g3", tag="big")
+        g4 = big.tile([P, PACK, S], F32, name="g4", tag="big")
+
+        h_first = work.tile([P, S], F32, name="h", tag="h")
+        sines = []
+        for h in range(2):
+            acc = psum.tile([P, HALF], F32, name="acc", tag="G")
+            for a in range(PASSES):
+                nc.tensor.matmul_mx(
+                    out=acc[:],
+                    lhsT=w1_codes[a][:, 0:P].bitcast(FP8X4),
+                    lhsT_scale=w1_sc[a][:, 0:P],
+                    rhs=v_codes[a][:, cols(h)].bitcast(FP8X4),
+                    rhs_scale=v_sc[4 * a : P, cols(h)],
+                    start=(a == 0),
+                    stop=(a == PASSES - 1),
+                )
+            whole = work.tile([P, HALF], I32, name="whole", tag="whole")
+            nc.vector.tensor_scalar(whole[:], acc[:], 1.0 / TWO_PI, None, ALU.mult)
+            frac = work.tile([P, HALF], F32, name="frac", tag="turns")
+            nc.vector.scalar_tensor_tensor(frac[:], acc[:], 1.0 / TWO_PI, whole[:], ALU.mult, ALU.subtract)
+            sine = work.tile([P, HALF], F32, name="sine", tag="sine")
+            nc.scalar.activation(sine[:], frac[:], ACT.Sin, bias=zero[:], scale=TWO_PI)
+            sines.append(sine)
+        quantise_w1_rest(PASSES - 1, last_rest)
+        for h in range(2):
+            nc.vector.scalar_tensor_tensor(
+                h_first[:, cols(h)], sines[h][:], gain_sb[:, 0:1], base_sb[0][:, cols(h)], ALU.mult, ALU.add
+            )
+            nc.vector.tensor_tensor(
+                page[0][:].indirect(entries(lists[1], h)), h_first[:, cols(h)], wgs_sb[0][:, cols(h)], ALU.mult
+            )
+        nc.vector.tensor_copy(g3[:, 0, :], page[0][:].indirect(lists[2][:]))
+        nc.vector.tensor_copy(g4[:, 0, :], page[0][:].indirect(lists[3][:]))
+
+        def add_turned(dst, parts):
+            for b in range(HALF // P):
+                for i, part in enumerate(parts):
+                    nc.tensor.matmul(
+                        dst[:, block(b)], part[:, block(b)], ident[:],
+                        is_transpose=True, start=(i == 0), stop=(i == len(parts) - 1),
+                    )
+
+        for t in range(1, PACK):
+            h_t = work.tile([P, S], F32, name="h", tag="h")
+            for h in range(2):
+                acc = psum.tile([P, HALF], F32, name="acc", tag="S")
+                for b in range(HALF // P):
+                    j = slice(h * HALF + b * P, h * HALF + (b + 1) * P)
+                    for a in range(PASSES):
+                        nc.tensor.matmul_mx(
+                            out=acc[:, block(b)],
+                            lhsT=v_codes[a][:, j].bitcast(FP8X4),
+                            lhsT_scale=v_sc[4 * a : P, j],
+                            rhs=w1_codes[a][:, block(t)].bitcast(FP8X4),
+                            rhs_scale=w1_sc[a][:, block(t)],
+                            start=(a == 0),
+                            stop=(a == PASSES - 1),
+                        )
+                whole = work.tile([P, HALF], U32, name="whole", tag="whole")
+                nc.scalar.activation(whole[:], acc[:], ACT.Copy, bias=ROUNDER, scale=1.0 / TWO_PI)
+                turns = work.tile([P, HALF], F32, name="turns", tag="turns")
+                nc.scalar.activation(turns[:], acc[:], ACT.Copy, scale=1.0 / TWO_PI)
+                minus = work.tile([P, HALF], F32, name="minus", tag="minus")
+                nc.scalar.activation(minus[:], whole[:], ACT.Copy, bias=ROUNDER, scale=-1.0)
+                frac = psum.tile([P, HALF], F32, name="frac", tag="R")
+                add_turned(frac, (turns, minus))
+                sine = work.tile([P, HALF], F32, name="sine", tag="sine")
+                nc.scalar.activation(sine[:], frac[:], ACT.Sin, bias=zero[:], scale=TWO_PI)
+                nc.scalar.activation(sine[:], sine[:], ACT.Copy, scale=gain_sb[:, t : t + 1])
+                summed = psum.tile([P, HALF], F32, name="summed", tag="G")
+                add_turned(summed, (sine, base_sb[t][:, cols(h)]))
+                turned = work.tile([P, HALF], F32, name="turned", tag="turned", align_bytes=64)
+                nc.scalar.copy(turned[:], summed[:])
+                back = psum.tile([P, HALF], F32, name="back", tag="H")
+                add_turned(back, (turned,))
+                nc.scalar.copy(h_t[:, cols(h)], back[:])
+            nc.vector.tensor_tensor(page[t][:].indirect(lists[1][:]), h_t[:], wgs_sb[t], ALU.mult)
+            if t < PACK - 1:
+                nc.vector.tensor_copy(g3[:, t, :], page[t][:].indirect(lists[2][:]))
+            else:
+                for h in range(2):
+                    nc.vector.tensor_copy(g3[:, t, cols(h)], page[t][:].indirect(entries(lists[2], h)))
+            nc.vector.tensor_copy(g4[:, t, :], page[t][:].indirect(lists[3][:]))
+
+        x = [work.tile([P, HALF, PACK], BF16, name="x", tag="turned", align_bytes=64) for h in range(2)]
+        for t in range(PACK):
+            for h in range(2):
+                nc.scalar.activation(
+                    x[h][:, :, t], g3[:, t, cols(h)], ACT.Abs, bias=zero[:], scale=sens_sb[:, t : t + 1]
+                )
+        x_codes = [keep.tile([P, HALF], U32, name=f"x_codes{h}", align_bytes=64) for h in range(2)]
+        x_sc = [keep.tile([P, HALF], U8, name=f"x_sc{h}", align_bytes=64) for h in range(2)]
+        for h in range(2):
+            nc.vector.quantize_mx(
+                out=x_codes[h][:].bitcast(FP8X4), scales=x_sc[h][:], in_=x[h][:].rearrange("p j t -> p (j t)")
+            )
+        for h in range(2):
+            for t in range(PACK):
+                y = psum.tile([P, HALF], F32, name="y", tag="SRGH"[t])
+                nc.tensor.matmul_mx(
+                    out=y[:],
+                    lhsT=w2_dealt[:, 2 * P * t : 2 * P * (t + 1)].bitcast(FP4X4),
+                    lhsT_scale=w2_sc[:, block(t)],
+                    rhs=x_codes[h][:].bitcast(FP8X4),
+                    rhs_scale=x_sc[h][:],
+                    start=True,
+                    stop=True,
+                )
+                nc.vector.scalar_tensor_tensor(
+                    g4[:, t, cols(h)], g4[:, t, cols(h)], refs_sb[:, t : t + 1], y[:], ALU.mult, ALU.max
+                )
+                nc.sync.dma_start(out=out_t[t][:, cols(h)], in_=g4[:, t, cols(h)])

@@ -33,7 +33,7 @@ def tile_list_bogie_vibration_page_kernel(
     nc = tc.nc
     with ExitStack() as ctx:
         keep = ctx.enter_context(tc.tile_pool(name="keep", bufs=1))
-        big = ctx.enter_context(tc.tile_pool(name="big", bufs=3))
+        big = ctx.enter_context(tc.tile_pool(name="big", bufs=2))
         work = ctx.enter_context(tc.tile_pool(name="work", bufs=2))
         psum = ctx.enter_context(tc.psum_pool(name="psum", bufs=2))
 
@@ -47,16 +47,16 @@ def tile_list_bogie_vibration_page_kernel(
             return slice(b * P, (b + 1) * P)
 
         lists = [keep.tile([P, S // 16], U16, name=f"list{i}") for i in range(4)]
-        tab_sc = keep.tile([P, T], U8, name="tab_sc")
-        w2_sc_raw = keep.tile([P, H], U8, name="w2_sc_raw")
-        nc.vector.memset(tab_sc[:].bitcast(I32), 0)
+        tab_sc = keep.tile([P, T], U8, name="tab_sc", tag="then_v2", align_bytes=64)
+        w2_sc_raw = keep.tile([P, H], U8, name="w2_sc_raw", tag="then_v0", align_bytes=64)
         nc.vector.memset(w2_sc_raw[:].bitcast(I32), 0)
+        nc.vector.memset(tab_sc[:].bitcast(I32), 0)
         zero_in = keep.tile([P, 1], F32, name="zero_in")
         zero = keep.tile([P, 1], F32, name="zero")
         nc.vector.memset(zero_in[:], 0.0)
         nc.scalar.activation(zero[:], zero_in[:], ACT.Sin, bias=zero_in[:])
 
-        w2_raw = keep.tile([P, 2 * H], U8, name="w2_raw")
+        w2_raw = keep.tile([P, 2 * H], U8, name="w2_raw", tag="then_v1", align_bytes=64)
         gain_sb = keep.tile([P, PACK], F32, name="gain_sb")
         sens_sb = keep.tile([P, PACK], F32, name="sens_sb")
         refs_sb = keep.tile([P, PACK], F32, name="refs_sb")
@@ -64,45 +64,36 @@ def tile_list_bogie_vibration_page_kernel(
         make_identity(nc, ident[:])
 
         w1_raw = [keep.tile([P, PACK, H], F32, name=f"w1_raw{a}") for a in range(PASSES)]
-        tab = [big.tile([P, T], U32, name=f"tab{a}", tag="big") for a in range(PASSES)]
+        tab = [big.tile([P, T], U32, name=f"tab{a}", tag="big") for a in range(PASSES - 1)]
+        tab.append(keep.tile([P, T], U32, name="tab2", tag="w1_first2", align_bytes=64))
 
         def load_w1(a):
             rows = w1[a * P * PACK : (a + 1) * P * PACK, :]
             nc.sync.dma_start(out=w1_raw[a][:], in_=rows.rearrange("(p j) c -> p j c", j=PACK))
 
-        def load_tab(a, half):
-            words = tab_words[a].rearrange("p n i -> p (n i)").bitcast(I32)
-            c = slice(half * T // 2, (half + 1) * T // 2)
-            nc.sync.dma_start(out=tab[a][:].bitcast(I32)[:, c], in_=words[:, c])
-
         def load_vec(dst, src):
             nc.sync.dma_start(out=dst[:], in_=src.rearrange("(p t) -> p t", t=PACK))
 
-        def load_tab_sc(q):
-            nc.sync.dma_start(
+        for q in range(4):
+            nc.gpsimd.dma_start(
+                out=w2_sc_raw[32 * q : 32 * q + 4, :].bitcast(I32),
+                in_=w2_scales[0, 4 * q : 4 * q + 4, :].bitcast(I32),
+            )
+        for q in range(4):
+            nc.gpsimd.dma_start(
                 out=tab_sc[32 * q : 32 * q + 4 * PASSES, :].bitcast(I32),
                 in_=tab_scales[:, 4 * q : 4 * q + 4, :].bitcast(I32),
             )
 
-        def load_w2_sc(q):
-            nc.sync.dma_start(
-                out=w2_sc_raw[32 * q : 32 * q + 4, :].bitcast(I32),
-                in_=w2_scales[0, 4 * q : 4 * q + 4, :].bitcast(I32),
-            )
-
         nc.sync.dma_start(lists[0][:], offs)
         load_w1(0)
-        load_w1(1)
         nc.sync.dma_start(out=w2_raw[:].bitcast(I32), in_=w2_words[0].bitcast(I32))
-        load_tab(0, 0)
-        load_vec(gain_sb, gain)
-        load_tab(0, 1)
-        load_vec(sens_sb, sens)
-        for a, load_sc in ((1, load_tab_sc), (2, load_w2_sc)):
-            for half in range(2):
-                load_sc(2 * half)
-                load_sc(2 * half + 1)
-                load_tab(a, half)
+        load_w1(1)
+        for a in range(PASSES):
+            nc.sync.dma_start(
+                out=tab[a][:].bitcast(I32),
+                in_=tab_words[a].rearrange("p n i -> p (n i)").bitcast(I32),
+            )
         load_w1(2)
 
         base_t = base.rearrange("(p t) j -> t p j", t=PACK)
@@ -111,37 +102,39 @@ def tile_list_bogie_vibration_page_kernel(
         wgs_q = wgs.rearrange("(q t) j -> q t j", t=PACK)
         base_sb = [keep.tile([P, S], F32, name=f"base{t}") for t in range(PACK)]
         page = [keep.tile([P, T2], F32, name=f"page{t}") for t in range(PACK)]
-        wgs_first = keep.tile([P, S], F32, name="wgs_first")
-        wgs_rest = keep.tile([P, PACK - 1, S], F32, name="wgs_rest")
-        wgs_sb = [wgs_first[:]] + [wgs_rest[:, t, :] for t in range(PACK - 1)]
+        wgs_sb = [keep.tile([P, S], F32, name=f"wgs{t}") for t in range(PACK)]
 
-        nc.sync.dma_start(out=base_sb[0][:], in_=base_t[0])
+        def load_wgs(t, c):
+            for g in range(4):
+                nc.sync.dma_start(out=wgs_sb[t][32 * g : 32 * g + 32, c], in_=wgs_q[:, t, c])
+
+        nc.sync.dma_start(out=base_sb[0][:, cols(0)], in_=base_t[0][:, cols(0)])
+        load_vec(gain_sb, gain)
         nc.sync.dma_start(lists[1][:], offs2)
-        for g in range(4):
-            nc.sync.dma_start(out=wgs_first[32 * g : 32 * g + 32, :], in_=wgs_q[:, 0, :])
+        load_wgs(0, cols(0))
         nc.sync.dma_start(out=page[0][:], in_=page_t[0])
-        nc.sync.dma_start(out=base_sb[1][:], in_=base_t[1])
-        load_vec(refs_sb, refs)
+        nc.sync.dma_start(out=base_sb[0][:, cols(1)], in_=base_t[0][:, cols(1)])
+        load_wgs(0, cols(1))
         nc.sync.dma_start(lists[2][:], offs3)
         nc.sync.dma_start(lists[3][:], offs4)
-        for g in range(4):
-            nc.sync.dma_start(out=wgs_rest[32 * g : 32 * g + 32, :, :], in_=wgs_q[:, 1:PACK, :])
-        nc.sync.dma_start(out=page[1][:], in_=page_t[1])
-        for t in range(2, PACK):
+        for t in range(1, PACK):
             nc.sync.dma_start(out=base_sb[t][:], in_=base_t[t])
+            load_wgs(t, slice(0, S))
             nc.sync.dma_start(out=page[t][:], in_=page_t[t])
+        load_vec(sens_sb, sens)
+        load_vec(refs_sb, refs)
 
         w2_dealt = keep.tile([P, 2 * H], U8, name="w2_dealt", align_bytes=64)
         w2_sc = keep.tile([P, H], U8, name="w2_sc", align_bytes=64)
 
         w1_codes = [keep.tile([P, H], U32, name=f"w1_codes{a}", align_bytes=64) for a in range(PASSES)]
         w1_sc = [keep.tile([P, H], U8, name=f"w1_sc{a}", align_bytes=64) for a in range(PASSES)]
-        v_codes = [keep.tile([P, S], U32, name=f"v_codes{a}", align_bytes=64) for a in range(PASSES)]
+        v_codes = [keep.tile([P, S], U32, name=f"v_codes{a}", tag=f"then_v{a}", align_bytes=64) for a in range(PASSES)]
         v_sc = keep.tile([P, S], U8, name="v_sc", align_bytes=64)
 
         def quantise_w1(a):
             src = w1_raw[a][:].rearrange("p j (m t) -> p m t j", t=PACK)
-            first = keep.tile([P, H], BF16, name=f"w1_first{a}", align_bytes=64)
+            first = keep.tile([P, H], BF16, name=f"w1_first{a}", tag=f"w1_first{a}", align_bytes=64)
             rest = keep.tile([P, (PACK - 1) * H], BF16, name=f"w1_rest{a}", align_bytes=64)
             nc.vector.tensor_copy(out=first[:].rearrange("p (m j) -> p m j", j=PACK), in_=src[:, :, 0, :])
             nc.scalar.copy(
@@ -160,9 +153,6 @@ def tile_list_bogie_vibration_page_kernel(
 
         for a in range(PASSES - 1):
             quantise_w1_rest(a, quantise_w1(a))
-        nc.vector.tensor_copy(v_codes[0][:], tab[0][:].indirect(lists[0][:]))
-        nc.vector.tensor_copy(v_sc[:], tab_sc[:].indirect(lists[0][:]))
-        nc.vector.tensor_copy(v_codes[1][:], tab[1][:].indirect(lists[0][:]))
         nc.vector.tensor_copy(
             out=w2_dealt[:].rearrange("p (t m b) -> p t m b", t=PACK, b=2),
             in_=w2_raw[:].rearrange("p (m t b) -> p t m b", t=PACK, b=2),
@@ -171,6 +161,9 @@ def tile_list_bogie_vibration_page_kernel(
             out=w2_sc[:].rearrange("p (t m) -> p t m", t=PACK),
             in_=w2_sc_raw[:].rearrange("p (m t) -> p t m", t=PACK),
         )
+        nc.vector.tensor_copy(v_codes[0][:], tab[0][:].indirect(lists[0][:]))
+        nc.vector.tensor_copy(v_sc[:], tab_sc[:].indirect(lists[0][:]))
+        nc.vector.tensor_copy(v_codes[1][:], tab[1][:].indirect(lists[0][:]))
         nc.vector.tensor_copy(v_codes[2][:], tab[2][:].indirect(lists[0][:]))
         last_rest = quantise_w1(PASSES - 1)
 
@@ -251,7 +244,7 @@ def tile_list_bogie_vibration_page_kernel(
                 back = psum.tile([P, HALF], F32, name="back", tag="H")
                 add_turned(back, (turned,))
                 nc.scalar.copy(h_t[:, cols(h)], back[:])
-            nc.vector.tensor_tensor(page[t][:].indirect(lists[1][:]), h_t[:], wgs_sb[t], ALU.mult)
+            nc.vector.tensor_tensor(page[t][:].indirect(lists[1][:]), h_t[:], wgs_sb[t][:], ALU.mult)
             if t < PACK - 1:
                 nc.vector.tensor_copy(g3[:, t, :], page[t][:].indirect(lists[2][:]))
             else:

@@ -33,7 +33,7 @@ def tile_list_bogie_vibration_page_kernel(
     nc = tc.nc
     with ExitStack() as ctx:
         keep = ctx.enter_context(tc.tile_pool(name="keep", bufs=1))
-        big = ctx.enter_context(tc.tile_pool(name="big", bufs=2))
+        big = ctx.enter_context(tc.tile_pool(name="big", bufs=3))
         work = ctx.enter_context(tc.tile_pool(name="work", bufs=2))
         psum = ctx.enter_context(tc.psum_pool(name="psum", bufs=2))
 
@@ -64,8 +64,7 @@ def tile_list_bogie_vibration_page_kernel(
         make_identity(nc, ident[:])
 
         w1_raw = [keep.tile([P, PACK, H], F32, name=f"w1_raw{a}") for a in range(PASSES)]
-        tab = [big.tile([P, T], U32, name=f"tab{a}", tag="big") for a in range(PASSES - 1)]
-        tab.append(keep.tile([P, T], U32, name="tab2", tag="w1_first2", align_bytes=64))
+        tab = [big.tile([P, T], U32, name=f"tab{a}", tag="big") for a in range(PASSES)]
 
         def load_w1(a):
             rows = w1[a * P * PACK : (a + 1) * P * PACK, :]
@@ -89,12 +88,12 @@ def tile_list_bogie_vibration_page_kernel(
         load_w1(0)
         nc.sync.dma_start(out=w2_raw[:].bitcast(I32), in_=w2_words[0].bitcast(I32))
         load_w1(1)
+        load_w1(2)
         for a in range(PASSES):
             nc.sync.dma_start(
                 out=tab[a][:].bitcast(I32),
                 in_=tab_words[a].rearrange("p n i -> p (n i)").bitcast(I32),
             )
-        load_w1(2)
 
         base_t = base.rearrange("(p t) j -> t p j", t=PACK)
         page_t = page0.rearrange("(p t) m -> t p m", t=PACK)
@@ -132,27 +131,13 @@ def tile_list_bogie_vibration_page_kernel(
         v_codes = [keep.tile([P, S], U32, name=f"v_codes{a}", tag=f"then_v{a}", align_bytes=64) for a in range(PASSES)]
         v_sc = keep.tile([P, S], U8, name="v_sc", align_bytes=64)
 
-        def quantise_w1(a):
-            src = w1_raw[a][:].rearrange("p j (m t) -> p m t j", t=PACK)
-            first = keep.tile([P, H], BF16, name=f"w1_first{a}", tag=f"w1_first{a}", align_bytes=64)
-            rest = keep.tile([P, (PACK - 1) * H], BF16, name=f"w1_rest{a}", align_bytes=64)
-            nc.vector.tensor_copy(out=first[:].rearrange("p (m j) -> p m j", j=PACK), in_=src[:, :, 0, :])
+        for a in range(PASSES):
+            grouped = keep.tile([P, PACK * H], BF16, name=f"w1_grouped{a}", align_bytes=64)
             nc.scalar.copy(
-                out=rest[:].rearrange("p (t m j) -> p m t j", t=PACK - 1, j=PACK), in_=src[:, :, 1:PACK, :]
+                out=grouped[:].rearrange("p (t m j) -> p m t j", t=PACK, j=PACK),
+                in_=w1_raw[a][:].rearrange("p j (m t) -> p m t j", t=PACK),
             )
-            nc.vector.quantize_mx(out=w1_codes[a][:, 0:P].bitcast(FP8X4), scales=w1_sc[a][:, 0:P], in_=first[:])
-            return rest
-
-        def quantise_w1_rest(a, rest):
-            for lo, hi in ((1, 2), (2, 4)):
-                nc.vector.quantize_mx(
-                    out=w1_codes[a][:, lo * P : hi * P].bitcast(FP8X4),
-                    scales=w1_sc[a][:, lo * P : hi * P],
-                    in_=rest[:, (lo - 1) * H : (hi - 1) * H],
-                )
-
-        for a in range(PASSES - 1):
-            quantise_w1_rest(a, quantise_w1(a))
+            nc.vector.quantize_mx(out=w1_codes[a][:].bitcast(FP8X4), scales=w1_sc[a][:], in_=grouped[:])
         nc.vector.tensor_copy(
             out=w2_dealt[:].rearrange("p (t m b) -> p t m b", t=PACK, b=2),
             in_=w2_raw[:].rearrange("p (m t b) -> p t m b", t=PACK, b=2),
@@ -164,8 +149,8 @@ def tile_list_bogie_vibration_page_kernel(
         nc.vector.tensor_copy(v_codes[0][:], tab[0][:].indirect(lists[0][:]))
         nc.vector.tensor_copy(v_sc[:], tab_sc[:].indirect(lists[0][:]))
         nc.vector.tensor_copy(v_codes[1][:], tab[1][:].indirect(lists[0][:]))
-        nc.vector.tensor_copy(v_codes[2][:], tab[2][:].indirect(lists[0][:]))
-        last_rest = quantise_w1(PASSES - 1)
+        for h in range(2):
+            nc.vector.tensor_copy(v_codes[2][:, cols(h)], tab[2][:].indirect(entries(lists[0], h)))
 
         g3 = big.tile([P, PACK, S], F32, name="g3", tag="big")
         g4 = big.tile([P, PACK, S], F32, name="g4", tag="big")
@@ -188,10 +173,9 @@ def tile_list_bogie_vibration_page_kernel(
             nc.vector.tensor_scalar(whole[:], acc[:], 1.0 / TWO_PI, None, ALU.mult)
             frac = work.tile([P, HALF], F32, name="frac", tag="turns")
             nc.vector.scalar_tensor_tensor(frac[:], acc[:], 1.0 / TWO_PI, whole[:], ALU.mult, ALU.subtract)
-            sine = work.tile([P, HALF], F32, name="sine", tag="sine")
+            sine = keep.tile([P, HALF], F32, name=f"sine0{h}")
             nc.scalar.activation(sine[:], frac[:], ACT.Sin, bias=zero[:], scale=TWO_PI)
             sines.append(sine)
-        quantise_w1_rest(PASSES - 1, last_rest)
         for h in range(2):
             nc.vector.scalar_tensor_tensor(
                 h_first[:, cols(h)], sines[h][:], gain_sb[:, 0:1], base_sb[0][:, cols(h)], ALU.mult, ALU.add
@@ -234,8 +218,16 @@ def tile_list_bogie_vibration_page_kernel(
                 nc.scalar.activation(minus[:], whole[:], ACT.Copy, bias=ROUNDER, scale=-1.0)
                 frac = psum.tile([P, HALF], F32, name="frac", tag="R")
                 add_turned(frac, (turns, minus))
-                sine = work.tile([P, HALF], F32, name="sine", tag="sine")
+                if t == 1:
+                    sine = keep.tile([P, HALF], F32, name=f"sine1{h}")
+                else:
+                    sine = work.tile([P, HALF], F32, name="sine", tag="sine")
                 nc.scalar.activation(sine[:], frac[:], ACT.Sin, bias=zero[:], scale=TWO_PI)
+                if t == 1:
+                    nc.vector.scalar_tensor_tensor(
+                        h_t[:, cols(h)], sine[:], gain_sb[:, t : t + 1], base_sb[t][:, cols(h)], ALU.mult, ALU.add
+                    )
+                    continue
                 nc.scalar.activation(sine[:], sine[:], ACT.Copy, scale=gain_sb[:, t : t + 1])
                 summed = psum.tile([P, HALF], F32, name="summed", tag="G")
                 add_turned(summed, (sine, base_sb[t][:, cols(h)]))

@@ -21,9 +21,12 @@ ACT = mybir.ActivationFunctionType
 P = 128
 PACK = 4
 PASSES = K // (P * PACK)
+QUADS, QUAD = 4, 32
 HALF = 512
 TWO_PI = 2.0 * math.pi
 ROUNDER = 1.5 * 2.0**23
+
+BASE_ON_VECTOR = ((0, 1), (1, 1))
 
 
 def tile_list_bogie_vibration_page_kernel(
@@ -33,89 +36,82 @@ def tile_list_bogie_vibration_page_kernel(
     nc = tc.nc
     with ExitStack() as ctx:
         keep = ctx.enter_context(tc.tile_pool(name="keep", bufs=1))
-        big = ctx.enter_context(tc.tile_pool(name="big", bufs=3))
+        big = ctx.enter_context(tc.tile_pool(name="big", bufs=PASSES))
         work = ctx.enter_context(tc.tile_pool(name="work", bufs=2))
         psum = ctx.enter_context(tc.psum_pool(name="psum", bufs=2))
 
-        def cols(h):
-            return slice(h * HALF, (h + 1) * HALF)
+        def cols(half):
+            return slice(half * HALF, (half + 1) * HALF)
 
-        def entries(lst, h):
-            return lst[:, h * HALF // 16 : (h + 1) * HALF // 16]
+        def entries(offsets, half):
+            return offsets[:, half * HALF // 16 : (half + 1) * HALF // 16]
 
         def block(b):
             return slice(b * P, (b + 1) * P)
 
-        lists = [keep.tile([P, S // 16], U16, name=f"list{i}") for i in range(4)]
-        tab_sc = keep.tile([P, T], U8, name="tab_sc", tag="then_v2", align_bytes=64)
-        w2_sc_raw = keep.tile([P, H], U8, name="w2_sc_raw", tag="then_v0", align_bytes=64)
-        nc.vector.memset(w2_sc_raw[:].bitcast(I32), 0)
+        w2_raw = keep.tile([P, 2 * H], U8, name="w2_raw", tag="before_v0", align_bytes=64)
+        tab_sc = keep.tile([P, T], U8, name="tab_sc", tag="before_v1", align_bytes=64)
+        w2_sc_raw = keep.tile([P, H], U8, name="w2_sc_raw", tag="before_v2", align_bytes=64)
         nc.vector.memset(tab_sc[:].bitcast(I32), 0)
+        nc.vector.memset(w2_sc_raw[:].bitcast(I32), 0)
+
         zero_in = keep.tile([P, 1], F32, name="zero_in")
         zero = keep.tile([P, 1], F32, name="zero")
         nc.vector.memset(zero_in[:], 0.0)
         nc.scalar.activation(zero[:], zero_in[:], ACT.Sin, bias=zero_in[:])
-
-        w2_raw = keep.tile([P, 2 * H], U8, name="w2_raw", tag="then_v1", align_bytes=64)
-        gain_sb = keep.tile([P, PACK], F32, name="gain_sb")
-        sens_sb = keep.tile([P, PACK], F32, name="sens_sb")
-        refs_sb = keep.tile([P, PACK], F32, name="refs_sb")
         ident = keep.tile([P, P], F32, name="ident")
         make_identity(nc, ident[:])
 
+        for q in range(QUADS):
+            nc.gpsimd.dma_start(
+                out=tab_sc[QUAD * q : QUAD * q + 4 * PASSES, :].bitcast(I32),
+                in_=tab_scales[:, 4 * q : 4 * q + 4, :].bitcast(I32),
+            )
+        for q in range(QUADS):
+            nc.gpsimd.dma_start(
+                out=w2_sc_raw[QUAD * q : QUAD * q + 4, :].bitcast(I32),
+                in_=w2_scales[0, 4 * q : 4 * q + 4, :].bitcast(I32),
+            )
+
+        idx, idx2, idx3, idx4 = (keep.tile([P, S // 16], U16, name=f"idx{i}") for i in range(4))
         w1_raw = [keep.tile([P, PACK, H], F32, name=f"w1_raw{a}") for a in range(PASSES)]
         tab = [big.tile([P, T], U32, name=f"tab{a}", tag="big") for a in range(PASSES)]
-
-        def load_w1(a):
-            rows = w1[a * P * PACK : (a + 1) * P * PACK, :]
-            nc.sync.dma_start(out=w1_raw[a][:], in_=rows.rearrange("(p j) c -> p j c", j=PACK))
+        gain_sb = keep.tile([P, PACK], F32, name="gain_sb")
+        sens_sb = keep.tile([P, PACK], F32, name="sens_sb")
+        refs_sb = keep.tile([P, PACK], F32, name="refs_sb")
+        base_sb = [keep.tile([P, S], F32, name=f"base{t}") for t in range(PACK)]
+        page = [keep.tile([P, T2], F32, name=f"page{t}") for t in range(PACK)]
+        wgs_sb = [keep.tile([P, S], F32, name=f"wgs{t}") for t in range(PACK)]
+        base_t = base.rearrange("(p t) j -> t p j", t=PACK)
+        page_t = page0.rearrange("(p t) m -> t p m", t=PACK)
+        out_t = out.rearrange("(p t) j -> t p j", t=PACK)
+        wgs_q = wgs.rearrange("(q t) j -> q t j", t=PACK)
 
         def load_vec(dst, src):
             nc.sync.dma_start(out=dst[:], in_=src.rearrange("(p t) -> p t", t=PACK))
 
-        for q in range(4):
-            nc.gpsimd.dma_start(
-                out=w2_sc_raw[32 * q : 32 * q + 4, :].bitcast(I32),
-                in_=w2_scales[0, 4 * q : 4 * q + 4, :].bitcast(I32),
-            )
-        for q in range(4):
-            nc.gpsimd.dma_start(
-                out=tab_sc[32 * q : 32 * q + 4 * PASSES, :].bitcast(I32),
-                in_=tab_scales[:, 4 * q : 4 * q + 4, :].bitcast(I32),
-            )
+        def load_wgs(t, c):
+            for q in (0, 2, 1, 3):
+                nc.sync.dma_start(out=wgs_sb[t][QUAD * q : QUAD * (q + 1), c], in_=wgs_q[:, t, c])
 
-        nc.sync.dma_start(lists[0][:], offs)
-        load_w1(0)
+        nc.sync.dma_start(idx[:], offs)
         nc.sync.dma_start(out=w2_raw[:].bitcast(I32), in_=w2_words[0].bitcast(I32))
-        load_w1(1)
-        load_w1(2)
+        for a in range(PASSES):
+            rows = w1[a * P * PACK : (a + 1) * P * PACK, :]
+            nc.sync.dma_start(out=w1_raw[a][:], in_=rows.rearrange("(p i) c -> p i c", i=PACK))
         for a in range(PASSES):
             nc.sync.dma_start(
                 out=tab[a][:].bitcast(I32),
                 in_=tab_words[a].rearrange("p n i -> p (n i)").bitcast(I32),
             )
-
-        base_t = base.rearrange("(p t) j -> t p j", t=PACK)
-        page_t = page0.rearrange("(p t) m -> t p m", t=PACK)
-        out_t = out.rearrange("(p t) j -> t p j", t=PACK)
-        wgs_q = wgs.rearrange("(q t) j -> q t j", t=PACK)
-        base_sb = [keep.tile([P, S], F32, name=f"base{t}") for t in range(PACK)]
-        page = [keep.tile([P, T2], F32, name=f"page{t}") for t in range(PACK)]
-        wgs_sb = [keep.tile([P, S], F32, name=f"wgs{t}") for t in range(PACK)]
-
-        def load_wgs(t, c):
-            for g in range(4):
-                nc.sync.dma_start(out=wgs_sb[t][32 * g : 32 * g + 32, c], in_=wgs_q[:, t, c])
-
-        nc.sync.dma_start(out=base_sb[0][:, cols(0)], in_=base_t[0][:, cols(0)])
-        load_vec(gain_sb, gain)
-        nc.sync.dma_start(lists[1][:], offs2)
-        load_wgs(0, cols(0))
         nc.sync.dma_start(out=page[0][:], in_=page_t[0])
-        nc.sync.dma_start(out=base_sb[0][:, cols(1)], in_=base_t[0][:, cols(1)])
-        load_wgs(0, cols(1))
-        nc.sync.dma_start(lists[2][:], offs3)
-        nc.sync.dma_start(lists[3][:], offs4)
+        load_vec(gain_sb, gain)
+        nc.sync.dma_start(idx2[:], offs2)
+        for half in range(2):
+            nc.sync.dma_start(out=base_sb[0][:, cols(half)], in_=base_t[0][:, cols(half)])
+            load_wgs(0, cols(half))
+        nc.sync.dma_start(idx3[:], offs3)
+        nc.sync.dma_start(idx4[:], offs4)
         for t in range(1, PACK):
             nc.sync.dma_start(out=base_sb[t][:], in_=base_t[t])
             load_wgs(t, slice(0, S))
@@ -123,68 +119,35 @@ def tile_list_bogie_vibration_page_kernel(
         load_vec(sens_sb, sens)
         load_vec(refs_sb, refs)
 
-        w2_dealt = keep.tile([P, 2 * H], U8, name="w2_dealt", align_bytes=64)
-        w2_sc = keep.tile([P, H], U8, name="w2_sc", align_bytes=64)
-
         w1_codes = [keep.tile([P, H], U32, name=f"w1_codes{a}", align_bytes=64) for a in range(PASSES)]
         w1_sc = [keep.tile([P, H], U8, name=f"w1_sc{a}", align_bytes=64) for a in range(PASSES)]
-        v_codes = [keep.tile([P, S], U32, name=f"v_codes{a}", tag=f"then_v{a}", align_bytes=64) for a in range(PASSES)]
-        v_sc = keep.tile([P, S], U8, name="v_sc", align_bytes=64)
-
         for a in range(PASSES):
-            grouped = keep.tile([P, PACK * H], BF16, name=f"w1_grouped{a}", align_bytes=64)
+            grouped = keep.tile([P, PACK * H], BF16, name="grouped", tag=f"w1_grouped{a}", align_bytes=64)
             nc.scalar.copy(
-                out=grouped[:].rearrange("p (t m j) -> p m t j", t=PACK, j=PACK),
-                in_=w1_raw[a][:].rearrange("p j (m t) -> p m t j", t=PACK),
+                out=grouped[:].rearrange("p (t m i) -> p m t i", t=PACK, i=PACK),
+                in_=w1_raw[a][:].rearrange("p i (m t) -> p m t i", t=PACK),
             )
             nc.vector.quantize_mx(out=w1_codes[a][:].bitcast(FP8X4), scales=w1_sc[a][:], in_=grouped[:])
+
+        w2_dealt = keep.tile([P, 2 * H], U8, name="w2_dealt", align_bytes=64)
+        w2_sc = keep.tile([P, H], U8, name="w2_sc", align_bytes=64)
+        v_sc = keep.tile([P, S], U8, name="v_sc", align_bytes=64)
+        v_codes = [
+            keep.tile([P, S], U32, name=f"v_codes{a}", tag=f"before_v{a}", align_bytes=64) for a in range(PASSES)
+        ]
         nc.vector.tensor_copy(
             out=w2_dealt[:].rearrange("p (t m b) -> p t m b", t=PACK, b=2),
             in_=w2_raw[:].rearrange("p (m t b) -> p t m b", t=PACK, b=2),
         )
+        nc.vector.tensor_copy(v_codes[0][:], tab[0][:].indirect(idx[:]))
+        nc.vector.tensor_copy(v_sc[:], tab_sc[:].indirect(idx[:]))
+        nc.vector.tensor_copy(v_codes[1][:], tab[1][:].indirect(idx[:]))
         nc.vector.tensor_copy(
             out=w2_sc[:].rearrange("p (t m) -> p t m", t=PACK),
             in_=w2_sc_raw[:].rearrange("p (m t) -> p t m", t=PACK),
         )
-        nc.vector.tensor_copy(v_codes[0][:], tab[0][:].indirect(lists[0][:]))
-        nc.vector.tensor_copy(v_sc[:], tab_sc[:].indirect(lists[0][:]))
-        nc.vector.tensor_copy(v_codes[1][:], tab[1][:].indirect(lists[0][:]))
-        for h in range(2):
-            nc.vector.tensor_copy(v_codes[2][:, cols(h)], tab[2][:].indirect(entries(lists[0], h)))
-
-        g3 = big.tile([P, PACK, S], F32, name="g3", tag="big")
-        g4 = big.tile([P, PACK, S], F32, name="g4", tag="big")
-
-        h_first = work.tile([P, S], F32, name="h", tag="h")
-        sines = []
-        for h in range(2):
-            acc = psum.tile([P, HALF], F32, name="acc", tag="G")
-            for a in range(PASSES):
-                nc.tensor.matmul_mx(
-                    out=acc[:],
-                    lhsT=w1_codes[a][:, 0:P].bitcast(FP8X4),
-                    lhsT_scale=w1_sc[a][:, 0:P],
-                    rhs=v_codes[a][:, cols(h)].bitcast(FP8X4),
-                    rhs_scale=v_sc[4 * a : P, cols(h)],
-                    start=(a == 0),
-                    stop=(a == PASSES - 1),
-                )
-            whole = work.tile([P, HALF], I32, name="whole", tag="whole")
-            nc.vector.tensor_scalar(whole[:], acc[:], 1.0 / TWO_PI, None, ALU.mult)
-            frac = work.tile([P, HALF], F32, name="frac", tag="turns")
-            nc.vector.scalar_tensor_tensor(frac[:], acc[:], 1.0 / TWO_PI, whole[:], ALU.mult, ALU.subtract)
-            sine = keep.tile([P, HALF], F32, name=f"sine0{h}")
-            nc.scalar.activation(sine[:], frac[:], ACT.Sin, bias=zero[:], scale=TWO_PI)
-            sines.append(sine)
-        for h in range(2):
-            nc.vector.scalar_tensor_tensor(
-                h_first[:, cols(h)], sines[h][:], gain_sb[:, 0:1], base_sb[0][:, cols(h)], ALU.mult, ALU.add
-            )
-            nc.vector.tensor_tensor(
-                page[0][:].indirect(entries(lists[1], h)), h_first[:, cols(h)], wgs_sb[0][:, cols(h)], ALU.mult
-            )
-        nc.vector.tensor_copy(g3[:, 0, :], page[0][:].indirect(lists[2][:]))
-        nc.vector.tensor_copy(g4[:, 0, :], page[0][:].indirect(lists[3][:]))
+        for half in range(2):
+            nc.vector.tensor_copy(v_codes[2][:, cols(half)], tab[2][:].indirect(entries(idx, half)))
 
         def add_turned(dst, parts):
             for b in range(HALF // P):
@@ -194,81 +157,123 @@ def tile_list_bogie_vibration_page_kernel(
                         is_transpose=True, start=(i == 0), stop=(i == len(parts) - 1),
                     )
 
-        for t in range(1, PACK):
-            h_t = work.tile([P, S], F32, name="h", tag="h")
-            for h in range(2):
-                acc = psum.tile([P, HALF], F32, name="acc", tag="S")
-                for b in range(HALF // P):
-                    j = slice(h * HALF + b * P, h * HALF + (b + 1) * P)
-                    for a in range(PASSES):
-                        nc.tensor.matmul_mx(
-                            out=acc[:, block(b)],
-                            lhsT=v_codes[a][:, j].bitcast(FP8X4),
-                            lhsT_scale=v_sc[4 * a : P, j],
-                            rhs=w1_codes[a][:, block(t)].bitcast(FP8X4),
-                            rhs_scale=w1_sc[a][:, block(t)],
-                            start=(a == 0),
-                            stop=(a == PASSES - 1),
-                        )
-                whole = work.tile([P, HALF], U32, name="whole", tag="whole")
-                nc.scalar.activation(whole[:], acc[:], ACT.Copy, bias=ROUNDER, scale=1.0 / TWO_PI)
-                turns = work.tile([P, HALF], F32, name="turns", tag="turns")
-                nc.scalar.activation(turns[:], acc[:], ACT.Copy, scale=1.0 / TWO_PI)
-                minus = work.tile([P, HALF], F32, name="minus", tag="minus")
-                nc.scalar.activation(minus[:], whole[:], ACT.Copy, bias=ROUNDER, scale=-1.0)
-                frac = psum.tile([P, HALF], F32, name="frac", tag="R")
-                add_turned(frac, (turns, minus))
-                if t == 1:
-                    sine = keep.tile([P, HALF], F32, name=f"sine1{h}")
-                else:
-                    sine = work.tile([P, HALF], F32, name="sine", tag="sine")
-                nc.scalar.activation(sine[:], frac[:], ACT.Sin, bias=zero[:], scale=TWO_PI)
-                if t == 1:
-                    nc.vector.scalar_tensor_tensor(
-                        h_t[:, cols(h)], sine[:], gain_sb[:, t : t + 1], base_sb[t][:, cols(h)], ALU.mult, ALU.add
-                    )
-                    continue
-                nc.scalar.activation(sine[:], sine[:], ACT.Copy, scale=gain_sb[:, t : t + 1])
-                summed = psum.tile([P, HALF], F32, name="summed", tag="G")
-                add_turned(summed, (sine, base_sb[t][:, cols(h)]))
-                turned = work.tile([P, HALF], F32, name="turned", tag="turned", align_bytes=64)
-                nc.scalar.copy(turned[:], summed[:])
-                back = psum.tile([P, HALF], F32, name="back", tag="H")
-                add_turned(back, (turned,))
-                nc.scalar.copy(h_t[:, cols(h)], back[:])
-            nc.vector.tensor_tensor(page[t][:].indirect(lists[1][:]), h_t[:], wgs_sb[t][:], ALU.mult)
-            if t < PACK - 1:
-                nc.vector.tensor_copy(g3[:, t, :], page[t][:].indirect(lists[2][:]))
-            else:
-                for h in range(2):
-                    nc.vector.tensor_copy(g3[:, t, cols(h)], page[t][:].indirect(entries(lists[2], h)))
-            nc.vector.tensor_copy(g4[:, t, :], page[t][:].indirect(lists[3][:]))
-
-        x = [work.tile([P, HALF, PACK], BF16, name="x", tag="turned", align_bytes=64) for h in range(2)]
-        for t in range(PACK):
-            for h in range(2):
-                nc.scalar.activation(
-                    x[h][:, :, t], g3[:, t, cols(h)], ACT.Abs, bias=zero[:], scale=sens_sb[:, t : t + 1]
+        def sine_by_vector(t, half, sine):
+            s1 = psum.tile([P, HALF], F32, name="s1", tag="sum")
+            for a in range(PASSES):
+                nc.tensor.matmul_mx(
+                    out=s1[:],
+                    lhsT=w1_codes[a][:, block(t)].bitcast(FP8X4),
+                    lhsT_scale=w1_sc[a][:, block(t)],
+                    rhs=v_codes[a][:, cols(half)].bitcast(FP8X4),
+                    rhs_scale=v_sc[4 * a : P, cols(half)],
+                    start=(a == 0),
+                    stop=(a == PASSES - 1),
                 )
-        x_codes = [keep.tile([P, HALF], U32, name=f"x_codes{h}", align_bytes=64) for h in range(2)]
-        x_sc = [keep.tile([P, HALF], U8, name=f"x_sc{h}", align_bytes=64) for h in range(2)]
-        for h in range(2):
-            nc.vector.quantize_mx(
-                out=x_codes[h][:].bitcast(FP8X4), scales=x_sc[h][:], in_=x[h][:].rearrange("p j t -> p (j t)")
+            whole = keep.tile([P, HALF], I32, name="whole_signed")
+            nc.vector.tensor_scalar(whole[:], s1[:], 1.0 / TWO_PI, None, ALU.mult)
+            frac = keep.tile([P, HALF], F32, name="frac_sb")
+            nc.vector.scalar_tensor_tensor(frac[:], s1[:], 1.0 / TWO_PI, whole[:], ALU.mult, ALU.subtract)
+            nc.scalar.activation(sine[:], frac[:], ACT.Sin, bias=zero[:], scale=TWO_PI)
+
+        def sine_by_tensor(t, half, sine):
+            s1 = psum.tile([P, HALF], F32, name="s1", tag="s1")
+            for b in range(HALF // P):
+                j = slice(half * HALF + b * P, half * HALF + (b + 1) * P)
+                for a in range(PASSES):
+                    nc.tensor.matmul_mx(
+                        out=s1[:, block(b)],
+                        lhsT=v_codes[a][:, j].bitcast(FP8X4),
+                        lhsT_scale=v_sc[4 * a : P, j],
+                        rhs=w1_codes[a][:, block(t)].bitcast(FP8X4),
+                        rhs_scale=w1_sc[a][:, block(t)],
+                        start=(a == 0),
+                        stop=(a == PASSES - 1),
+                    )
+            shifted = work.tile([P, HALF], U32, name="shifted")
+            nc.scalar.activation(shifted[:], s1[:], ACT.Copy, bias=ROUNDER, scale=1.0 / TWO_PI)
+            turns = work.tile([P, HALF], F32, name="turns")
+            nc.scalar.activation(turns[:], s1[:], ACT.Copy, scale=1.0 / TWO_PI)
+            minus_whole = work.tile([P, HALF], F32, name="minus_whole")
+            nc.scalar.activation(minus_whole[:], shifted[:], ACT.Copy, bias=ROUNDER, scale=-1.0)
+            frac = psum.tile([P, HALF], F32, name="frac", tag="frac")
+            add_turned(frac, (turns, minus_whole))
+            nc.scalar.activation(sine[:], frac[:], ACT.Sin, bias=zero[:], scale=TWO_PI)
+
+        def base_by_vector(t, half, sine, h):
+            nc.vector.scalar_tensor_tensor(
+                h[:, cols(half)], sine[:], gain_sb[:, t : t + 1], base_sb[t][:, cols(half)], ALU.mult, ALU.add
             )
-        for h in range(2):
-            for t in range(PACK):
-                y = psum.tile([P, HALF], F32, name="y", tag="SRGH"[t])
+
+        def base_by_tensor(t, half, sine, h):
+            nc.scalar.activation(sine[:], sine[:], ACT.Copy, scale=gain_sb[:, t : t + 1])
+            summed = psum.tile([P, HALF], F32, name="summed", tag="sum")
+            add_turned(summed, (sine, base_sb[t][:, cols(half)]))
+            turned = work.tile([P, HALF], F32, name="turned", tag="turned")
+            nc.scalar.copy(turned[:], summed[:])
+            back = psum.tile([P, HALF], F32, name="back", tag="back")
+            add_turned(back, (turned,))
+            nc.scalar.copy(h[:, cols(half)], back[:])
+
+        picked3 = big.tile([P, PACK, S], F32, name="picked3", tag="big")
+        picked4 = big.tile([P, PACK, S], F32, name="picked4", tag="big")
+        for t in range(PACK):
+            h = work.tile([P, S], F32, name="h")
+            for half in range(2):
+                first = (t, half) == (0, 0)
+                if first or (t, half) in BASE_ON_VECTOR:
+                    sine = keep.tile([P, HALF], F32, name=f"sine{t}{half}")
+                    (sine_by_vector if first else sine_by_tensor)(t, half, sine)
+                    base_by_vector(t, half, sine, h)
+                else:
+                    sine = work.tile([P, HALF], F32, name="sine")
+                    sine_by_tensor(t, half, sine)
+                    base_by_tensor(t, half, sine, h)
+                if t == 0:
+                    nc.vector.tensor_tensor(
+                        page[t][:].indirect(entries(idx2, half)), h[:, cols(half)], wgs_sb[t][:, cols(half)], ALU.mult
+                    )
+            if t > 0:
+                nc.vector.tensor_tensor(page[t][:].indirect(idx2[:]), h[:], wgs_sb[t][:], ALU.mult)
+            if t < PACK - 1:
+                nc.vector.tensor_copy(picked3[:, t, :], page[t][:].indirect(idx3[:]))
+            else:
+                for half in range(2):
+                    nc.vector.tensor_copy(picked3[:, t, cols(half)], page[t][:].indirect(entries(idx3, half)))
+            nc.vector.tensor_copy(picked4[:, t, :], page[t][:].indirect(idx4[:]))
+
+        pairs = work.tile([P, 2, S, 2], BF16, name="pairs", tag="turned")
+        pair_words = pairs[:].rearrange("p u j e -> p u (j e)").bitcast(F32)
+
+        def magnitudes(t, c):
+            nc.scalar.activation(
+                pairs[:, t // 2, c, t % 2], picked3[:, t, c], ACT.Abs, bias=zero[:], scale=sens_sb[:, t : t + 1]
+            )
+
+        for t in range(PACK - 1):
+            magnitudes(t, slice(0, S))
+        x_codes = [keep.tile([P, HALF], U32, name=f"x_codes{half}", align_bytes=64) for half in range(2)]
+        x_sc = [keep.tile([P, HALF], U8, name=f"x_sc{half}", align_bytes=64) for half in range(2)]
+        for half in range(2):
+            magnitudes(PACK - 1, cols(half))
+            x = keep.tile([P, PACK * HALF], BF16, name="x", tag=f"w1_grouped{half}", align_bytes=64)
+            nc.scalar.copy(
+                out=x[:].bitcast(F32).rearrange("p (j u) -> p j u", u=2),
+                in_=pair_words[:, :, cols(half)].rearrange("p u j -> p j u"),
+            )
+            nc.vector.quantize_mx(out=x_codes[half][:].bitcast(FP8X4), scales=x_sc[half][:], in_=x[:])
+
+        for half in range(2):
+            for t, bank in enumerate(("s1", "frac", "sum", "back")):
+                y = psum.tile([P, HALF], F32, name="y", tag=bank)
                 nc.tensor.matmul_mx(
                     out=y[:],
                     lhsT=w2_dealt[:, 2 * P * t : 2 * P * (t + 1)].bitcast(FP4X4),
                     lhsT_scale=w2_sc[:, block(t)],
-                    rhs=x_codes[h][:].bitcast(FP8X4),
-                    rhs_scale=x_sc[h][:],
+                    rhs=x_codes[half][:].bitcast(FP8X4),
+                    rhs_scale=x_sc[half][:],
                     start=True,
                     stop=True,
                 )
-                nc.vector.scalar_tensor_tensor(
-                    g4[:, t, cols(h)], g4[:, t, cols(h)], refs_sb[:, t : t + 1], y[:], ALU.mult, ALU.max
-                )
-                nc.sync.dma_start(out=out_t[t][:, cols(h)], in_=g4[:, t, cols(h)])
+                result = picked4[:, t, cols(half)]
+                nc.vector.scalar_tensor_tensor(result, result, refs_sb[:, t : t + 1], y[:], ALU.mult, ALU.max)
+                nc.sync.dma_start(out=out_t[t][:, cols(half)], in_=result)

import math
from contextlib import ExitStack

import concourse.mybir as mybir
from concourse.masks import make_identity

K, T, S, H, T2 = 1536, 4096, 1024, 512, 2048
FLOPS = 2 * K * H * S + 2 * H * H * S

F32 = mybir.dt.float32
BF16 = mybir.dt.bfloat16
I32 = mybir.dt.int32
U32 = mybir.dt.uint32
U16 = mybir.dt.uint16
U8 = mybir.dt.uint8
FP8X4 = mybir.dt.float8_e4m3fn_x4
FP4X4 = mybir.dt.float4_e2m1fn_x4
ALU = mybir.AluOpType
ACT = mybir.ActivationFunctionType

P = 128
PACK = 4
PASSES = K // (P * PACK)
QUADS, QUAD = 4, 32
HALF = 512
TWO_PI = 2.0 * math.pi
ROUNDER = 1.5 * 2.0**23

BASE_ON_VECTOR = ((0, 1), (1, 1))


def tile_list_bogie_vibration_page_kernel(
    tc, tab_words, tab_scales, offs, offs2, offs3, offs4, w1, gain, base,
    wgs, page0, sens, w2_words, w2_scales, refs, out,
):
    nc = tc.nc
    with ExitStack() as ctx:
        keep = ctx.enter_context(tc.tile_pool(name="keep", bufs=1))
        big = ctx.enter_context(tc.tile_pool(name="big", bufs=PASSES))
        work = ctx.enter_context(tc.tile_pool(name="work", bufs=2))
        psum = ctx.enter_context(tc.psum_pool(name="psum", bufs=2))

        def cols(half):
            return slice(half * HALF, (half + 1) * HALF)

        def entries(offsets, half):
            return offsets[:, half * HALF // 16 : (half + 1) * HALF // 16]

        def block(b):
            return slice(b * P, (b + 1) * P)

        w2_raw = keep.tile([P, 2 * H], U8, name="w2_raw", tag="before_v0", align_bytes=64)
        tab_sc = keep.tile([P, T], U8, name="tab_sc", tag="before_v1", align_bytes=64)
        w2_sc_raw = keep.tile([P, H], U8, name="w2_sc_raw", tag="before_v2", align_bytes=64)
        nc.vector.memset(tab_sc[:].bitcast(I32), 0)
        nc.vector.memset(w2_sc_raw[:].bitcast(I32), 0)

        zero_in = keep.tile([P, 1], F32, name="zero_in")
        zero = keep.tile([P, 1], F32, name="zero")
        nc.vector.memset(zero_in[:], 0.0)
        nc.scalar.activation(zero[:], zero_in[:], ACT.Sin, bias=zero_in[:])
        ident = keep.tile([P, P], F32, name="ident")
        make_identity(nc, ident[:])

        for q in range(QUADS):
            nc.gpsimd.dma_start(
                out=tab_sc[QUAD * q : QUAD * q + 4 * PASSES, :].bitcast(I32),
                in_=tab_scales[:, 4 * q : 4 * q + 4, :].bitcast(I32),
            )
        for q in range(QUADS):
            nc.gpsimd.dma_start(
                out=w2_sc_raw[QUAD * q : QUAD * q + 4, :].bitcast(I32),
                in_=w2_scales[0, 4 * q : 4 * q + 4, :].bitcast(I32),
            )

        idx, idx2, idx3, idx4 = (keep.tile([P, S // 16], U16, name=f"idx{i}") for i in range(4))
        w1_raw = [keep.tile([P, PACK, H], F32, name=f"w1_raw{a}") for a in range(PASSES)]
        tab = [big.tile([P, T], U32, name=f"tab{a}", tag="big") for a in range(PASSES)]
        gain_sb = keep.tile([P, PACK], F32, name="gain_sb")
        sens_sb = keep.tile([P, PACK], F32, name="sens_sb")
        refs_sb = keep.tile([P, PACK], F32, name="refs_sb")
        base_sb = [keep.tile([P, S], F32, name=f"base{t}") for t in range(PACK)]
        page = [keep.tile([P, T2], F32, name=f"page{t}") for t in range(PACK)]
        wgs_sb = [keep.tile([P, S], F32, name=f"wgs{t}") for t in range(PACK)]
        base_t = base.rearrange("(p t) j -> t p j", t=PACK)
        page_t = page0.rearrange("(p t) m -> t p m", t=PACK)
        out_t = out.rearrange("(p t) j -> t p j", t=PACK)
        wgs_q = wgs.rearrange("(q t) j -> q t j", t=PACK)

        def load_vec(dst, src):
            nc.sync.dma_start(out=dst[:], in_=src.rearrange("(p t) -> p t", t=PACK))

        def load_wgs(t, c):
            for q in (0, 2, 1, 3):
                nc.sync.dma_start(out=wgs_sb[t][QUAD * q : QUAD * (q + 1), c], in_=wgs_q[:, t, c])

        nc.sync.dma_start(idx[:], offs)
        nc.sync.dma_start(out=w2_raw[:].bitcast(I32), in_=w2_words[0].bitcast(I32))
        for a in range(PASSES):
            rows = w1[a * P * PACK : (a + 1) * P * PACK, :]
            nc.sync.dma_start(out=w1_raw[a][:], in_=rows.rearrange("(p i) c -> p i c", i=PACK))
        for a in range(PASSES):
            nc.sync.dma_start(
                out=tab[a][:].bitcast(I32),
                in_=tab_words[a].rearrange("p n i -> p (n i)").bitcast(I32),
            )
        nc.sync.dma_start(out=page[0][:], in_=page_t[0])
        load_vec(gain_sb, gain)
        nc.sync.dma_start(idx2[:], offs2)
        for half in range(2):
            nc.sync.dma_start(out=base_sb[0][:, cols(half)], in_=base_t[0][:, cols(half)])
            load_wgs(0, cols(half))
        nc.sync.dma_start(idx3[:], offs3)
        nc.sync.dma_start(idx4[:], offs4)
        for t in range(1, PACK):
            nc.sync.dma_start(out=base_sb[t][:], in_=base_t[t])
            load_wgs(t, slice(0, S))
            nc.sync.dma_start(out=page[t][:], in_=page_t[t])
        load_vec(sens_sb, sens)
        load_vec(refs_sb, refs)

        w1_codes = [keep.tile([P, H], U32, name=f"w1_codes{a}", align_bytes=64) for a in range(PASSES)]
        w1_sc = [keep.tile([P, H], U8, name=f"w1_sc{a}", align_bytes=64) for a in range(PASSES)]
        for a in range(PASSES):
            grouped = keep.tile([P, PACK * H], BF16, name="grouped", tag=f"w1_grouped{a}", align_bytes=64)
            nc.scalar.copy(
                out=grouped[:].rearrange("p (t m i) -> p m t i", t=PACK, i=PACK),
                in_=w1_raw[a][:].rearrange("p i (m t) -> p m t i", t=PACK),
            )
            nc.vector.quantize_mx(out=w1_codes[a][:].bitcast(FP8X4), scales=w1_sc[a][:], in_=grouped[:])

        w2_dealt = keep.tile([P, 2 * H], U8, name="w2_dealt", align_bytes=64)
        w2_sc = keep.tile([P, H], U8, name="w2_sc", align_bytes=64)
        v_sc = keep.tile([P, S], U8, name="v_sc", align_bytes=64)
        v_codes = [
            keep.tile([P, S], U32, name=f"v_codes{a}", tag=f"before_v{a}", align_bytes=64) for a in range(PASSES)
        ]
        nc.vector.tensor_copy(
            out=w2_dealt[:].rearrange("p (t m b) -> p t m b", t=PACK, b=2),
            in_=w2_raw[:].rearrange("p (m t b) -> p t m b", t=PACK, b=2),
        )
        nc.vector.tensor_copy(v_codes[0][:], tab[0][:].indirect(idx[:]))
        nc.vector.tensor_copy(v_sc[:], tab_sc[:].indirect(idx[:]))
        nc.vector.tensor_copy(v_codes[1][:], tab[1][:].indirect(idx[:]))
        nc.vector.tensor_copy(
            out=w2_sc[:].rearrange("p (t m) -> p t m", t=PACK),
            in_=w2_sc_raw[:].rearrange("p (m t) -> p t m", t=PACK),
        )
        for half in range(2):
            nc.vector.tensor_copy(v_codes[2][:, cols(half)], tab[2][:].indirect(entries(idx, half)))

        def add_turned(dst, parts):
            for b in range(HALF // P):
                for i, part in enumerate(parts):
                    nc.tensor.matmul(
                        dst[:, block(b)], part[:, block(b)], ident[:],
                        is_transpose=True, start=(i == 0), stop=(i == len(parts) - 1),
                    )

        def sine_by_vector(t, half, sine):
            s1 = psum.tile([P, HALF], F32, name="s1", tag="sum")
            for a in range(PASSES):
                nc.tensor.matmul_mx(
                    out=s1[:],
                    lhsT=w1_codes[a][:, block(t)].bitcast(FP8X4),
                    lhsT_scale=w1_sc[a][:, block(t)],
                    rhs=v_codes[a][:, cols(half)].bitcast(FP8X4),
                    rhs_scale=v_sc[4 * a : P, cols(half)],
                    start=(a == 0),
                    stop=(a == PASSES - 1),
                )
            whole = keep.tile([P, HALF], I32, name="whole_signed")
            nc.vector.tensor_scalar(whole[:], s1[:], 1.0 / TWO_PI, None, ALU.mult)
            frac = keep.tile([P, HALF], F32, name="frac_sb")
            nc.vector.scalar_tensor_tensor(frac[:], s1[:], 1.0 / TWO_PI, whole[:], ALU.mult, ALU.subtract)
            nc.scalar.activation(sine[:], frac[:], ACT.Sin, bias=zero[:], scale=TWO_PI)

        def sine_by_tensor(t, half, sine):
            s1 = psum.tile([P, HALF], F32, name="s1", tag="s1")
            for b in range(HALF // P):
                j = slice(half * HALF + b * P, half * HALF + (b + 1) * P)
                for a in range(PASSES):
                    nc.tensor.matmul_mx(
                        out=s1[:, block(b)],
                        lhsT=v_codes[a][:, j].bitcast(FP8X4),
                        lhsT_scale=v_sc[4 * a : P, j],
                        rhs=w1_codes[a][:, block(t)].bitcast(FP8X4),
                        rhs_scale=w1_sc[a][:, block(t)],
                        start=(a == 0),
                        stop=(a == PASSES - 1),
                    )
            shifted = work.tile([P, HALF], U32, name="shifted")
            nc.scalar.activation(shifted[:], s1[:], ACT.Copy, bias=ROUNDER, scale=1.0 / TWO_PI)
            turns = work.tile([P, HALF], F32, name="turns")
            nc.scalar.activation(turns[:], s1[:], ACT.Copy, scale=1.0 / TWO_PI)
            minus_whole = work.tile([P, HALF], F32, name="minus_whole")
            nc.scalar.activation(minus_whole[:], shifted[:], ACT.Copy, bias=ROUNDER, scale=-1.0)
            frac = psum.tile([P, HALF], F32, name="frac", tag="frac")
            add_turned(frac, (turns, minus_whole))
            nc.scalar.activation(sine[:], frac[:], ACT.Sin, bias=zero[:], scale=TWO_PI)

        def base_by_vector(t, half, sine, h):
            nc.vector.scalar_tensor_tensor(
                h[:, cols(half)], sine[:], gain_sb[:, t : t + 1], base_sb[t][:, cols(half)], ALU.mult, ALU.add
            )

        def base_by_tensor(t, half, sine, h):
            nc.scalar.activation(sine[:], sine[:], ACT.Copy, scale=gain_sb[:, t : t + 1])
            summed = psum.tile([P, HALF], F32, name="summed", tag="sum")
            add_turned(summed, (sine, base_sb[t][:, cols(half)]))
            turned = work.tile([P, HALF], F32, name="turned", tag="turned")
            nc.scalar.copy(turned[:], summed[:])
            back = psum.tile([P, HALF], F32, name="back", tag="back")
            add_turned(back, (turned,))
            nc.scalar.copy(h[:, cols(half)], back[:])

        picked3 = big.tile([P, PACK, S], F32, name="picked3", tag="big")
        picked4 = big.tile([P, PACK, S], F32, name="picked4", tag="big")
        for t in range(PACK):
            h = work.tile([P, S], F32, name="h")
            for half in range(2):
                first = (t, half) == (0, 0)
                if first or (t, half) in BASE_ON_VECTOR:
                    sine = keep.tile([P, HALF], F32, name=f"sine{t}{half}")
                    (sine_by_vector if first else sine_by_tensor)(t, half, sine)
                    base_by_vector(t, half, sine, h)
                else:
                    sine = work.tile([P, HALF], F32, name="sine")
                    sine_by_tensor(t, half, sine)
                    base_by_tensor(t, half, sine, h)
                if t == 0:
                    nc.vector.tensor_tensor(
                        page[t][:].indirect(entries(idx2, half)), h[:, cols(half)], wgs_sb[t][:, cols(half)], ALU.mult
                    )
            if t > 0:
                nc.vector.tensor_tensor(page[t][:].indirect(idx2[:]), h[:], wgs_sb[t][:], ALU.mult)
            if t < PACK - 1:
                nc.vector.tensor_copy(picked3[:, t, :], page[t][:].indirect(idx3[:]))
            else:
                for half in range(2):
                    nc.vector.tensor_copy(picked3[:, t, cols(half)], page[t][:].indirect(entries(idx3, half)))
            nc.vector.tensor_copy(picked4[:, t, :], page[t][:].indirect(idx4[:]))

        pairs = work.tile([P, 2, S, 2], BF16, name="pairs", tag="turned")
        pair_words = pairs[:].rearrange("p u j e -> p u (j e)").bitcast(F32)

        def magnitudes(t, c):
            nc.scalar.activation(
                pairs[:, t // 2, c, t % 2], picked3[:, t, c], ACT.Abs, bias=zero[:], scale=sens_sb[:, t : t + 1]
            )

        for t in range(PACK - 1):
            magnitudes(t, slice(0, S))
        x_codes = [keep.tile([P, HALF], U32, name=f"x_codes{half}", align_bytes=64) for half in range(2)]
        x_sc = [keep.tile([P, HALF], U8, name=f"x_sc{half}", align_bytes=64) for half in range(2)]
        for half in range(2):
            magnitudes(PACK - 1, cols(half))
            x = keep.tile([P, PACK * HALF], BF16, name="x", tag=f"w1_grouped{half}", align_bytes=64)
            nc.scalar.copy(
                out=x[:].bitcast(F32).rearrange("p (j u) -> p j u", u=2),
                in_=pair_words[:, :, cols(half)].rearrange("p u j -> p j u"),
            )
            nc.vector.quantize_mx(out=x_codes[half][:].bitcast(FP8X4), scales=x_sc[half][:], in_=x[:])

        for half in range(2):
            for t, bank in enumerate(("s1", "frac", "sum", "back")):
                y = psum.tile([P, HALF], F32, name="y", tag=bank)
                nc.tensor.matmul_mx(
                    out=y[:],
                    lhsT=w2_dealt[:, 2 * P * t : 2 * P * (t + 1)].bitcast(FP4X4),
                    lhsT_scale=w2_sc[:, block(t)],
                    rhs=x_codes[half][:].bitcast(FP8X4),
                    rhs_scale=x_sc[half][:],
                    start=True,
                    stop=True,
                )
                result = picked4[:, t, cols(half)]
                nc.vector.scalar_tensor_tensor(result, result, refs_sb[:, t : t + 1], y[:], ALU.mult, ALU.max)
                nc.sync.dma_start(out=out_t[t][:, cols(half)], in_=result)
